import numpy as np
import ml_dtypes


def mxq(x, axis, fmt="e4m3"):
    dtype, down = {"e4m3": (ml_dtypes.float8_e4m3fn, 7), "e5m2": (ml_dtypes.float8_e5m2, 14)}[fmt]
    v = np.moveaxis(np.asarray(x, np.float32).astype(ml_dtypes.bfloat16).astype(np.float64), axis, -1)
    blocks = v.reshape(v.shape[:-1] + (-1, 32))
    amax = np.abs(blocks).max(-1, keepdims=True)
    byte = np.maximum(np.where(amax > 0, np.frexp(amax)[1] - 1 + 127, 0) - down, 1)
    scale = np.exp2(byte - 127.0)
    codes = (blocks / scale).astype(np.float32).astype(dtype).astype(np.float64)
    return np.moveaxis((codes * scale).reshape(v.shape), -1, axis)


WIDE = False


def mx_kscale(k):
    if not WIDE:
        return np.ones(k)
    levels = np.array([10, -10, 5, -5, 0])
    if k % 512:
        return np.exp2(np.random.permutation(np.resize(levels, k // 32))).repeat(32)
    a = np.empty((k // 512, 16))
    for p in range(k // 512):
        a[p, :8] = np.random.permutation(np.resize(levels, 8))
        for g in range(8):
            far = levels[np.abs(levels - a[p, g]) >= 10]
            a[p, g + 8] = far[np.random.randint(len(far))]
    return np.exp2(a.ravel()).repeat(32)


def f64(x):
    return np.asarray(x).astype(np.float64)


def striped(idx):
    return np.tile(idx.reshape(-1, 16).T, (8, 1)).astype(np.uint16)


def unstriped(offs):
    return offs[:16].T.reshape(-1).astype(np.int64)


def gelu(v):
    return 0.5 * v * (1.0 + np.tanh(np.sqrt(2.0 / np.pi) * (v + 0.044715 * v**3)))


K, T, E, C, H, N = 1024, 2048, 4, 128, 512, 256


def by_expert(wq, xq):
    return np.concatenate([wq[e].T @ xq[:, e * C:(e + 1) * C] for e in range(E)], axis=1)


def setup_inputs():
    n = np.random.standard_normal
    s = mx_kscale(K)[:, None]
    u = mx_kscale(H)
    return {
        "xT": (n((K, T)) * s).astype(np.float32),
        "w1": (n((E, K, H)) / np.sqrt(K) / s[None]).astype(np.float32),
        "w3": (n((E, K, H)) / np.sqrt(K) / s[None] * u[None, None, :]).astype(np.float32),
        "w2": (n((E, H, N)) / np.sqrt(H) / u[None, :, None]).astype(np.float32),
        "gate": np.tile(np.random.uniform(0.2, 1.0, E * C), (N, 1)).astype(np.float32),
        "offs": striped(np.random.permutation(T)[:E * C]),
    }


def reference(xT, w1, w3, w2, gate, offs):
    idx = unstriped(offs)
    xq = mxq(f64(xT)[:, idx], 0, "e4m3")
    h = gelu(by_expert(mxq(f64(w1), 1, "e4m3"), xq))
    h = h * by_expert(mxq(f64(w3), 1, "e4m3"), xq)
    y = by_expert(mxq(f64(w2), 1, "e4m3"), mxq(h, 0, "e4m3"))
    out = np.zeros((N, T))
    out[:, idx] = f64(gate) * y
    return out

@@ -1,0 +1,292 @@
+from contextlib import ExitStack
+
+import concourse.mybir as mybir
+
+K, T, E, C, H, N = 1024, 2048, 4, 128, 512, 256
+FLOPS = 2 * E * C * (2 * K * H + H * N)
+
+F32 = mybir.dt.float32
+BF16 = mybir.dt.bfloat16
+U32 = mybir.dt.uint32
+U16 = mybir.dt.uint16
+U8 = mybir.dt.uint8
+FP8X4 = mybir.dt.float8_e4m3fn_x4
+GELU = mybir.ActivationFunctionType.Gelu_apprx_tanh
+MULT = mybir.AluOpType.mult
+
+P = 128
+PACK = 4
+K_PASS = P * PACK
+PASSES = K // K_PASS
+SLOTS = E * C
+PAIR = 2 * C
+PAIRS = E // 2
+N_BLOCKS = N // P
+
+RING = 12
+CUT_W = (60, 60, 60, 60)
+CUT_W_LAST = 84
+CUT_X = 78
+CUT_W2 = (24, 24, 0, 0)
+SCATTER_STEPS = (1, 2)
+LAST_UNIT = ("w3", E - 1, PASSES - 1)
+DIRECT_UNITS = 5
+
+
+def shared_copy(nc, dst, src, cut):
+    rows = dst.shape[1]
+    if cut > 0:
+        nc.vector.tensor_copy(out=dst[:, :cut], in_=src[:, :cut])
+    if cut < rows:
+        nc.scalar.copy(out=dst[:, cut:], in_=src[:, cut:])
+
+
+def tile_routed_moe_kernel(tc, xT, w1, w3, w2, gate, offs, out):
+    nc = tc.nc
+    with ExitStack() as ctx:
+        held = ctx.enter_context(tc.tile_pool(name="held", bufs=1))
+        ring = ctx.enter_context(tc.tile_pool(name="ring", bufs=RING))
+        stage = ctx.enter_context(tc.tile_pool(name="stage", bufs=4))
+        work = ctx.enter_context(tc.tile_pool(name="work", bufs=2))
+        psum = ctx.enter_context(tc.psum_pool(name="psum", bufs=2))
+
+        offsets = held.tile([P, SLOTS // 16], U16, name="offsets")
+        nc.sync.dma_start(offsets[:], offs)
+
+        warm = held.tile([P, 2], F32, name="warm")
+        nc.vector.memset(warm[:], 0.0)
+        nc.scalar.activation(out=warm[:, 1:2], in_=warm[:, 0:1], func=GELU)
+
+        windows = []
+        for nb in range(N_BLOCKS):
+            window = held.tile([P, T], F32, name="window%d" % nb)
+            nc.vector.memset(window[:], 0.0)
+            windows.append(window)
+
+        x_planes = xT.rearrange("(g p t) n -> g t p n", p=P, t=PACK)
+        x_codes = []
+        x_scales = []
+        x_grouped = []
+        picked = []
+
+        def gather_plane(g, t):
+            plane = ring.tile([P, T], F32, name="plane", tag="raw")
+            nc.sync.dma_start(plane[:], x_planes[g, t])
+            nc.vector.tensor_copy(picked[g][:, t, :], plane[:].indirect(offsets[:]))
+
+        def interleave_tokens(g):
+            shared_copy(
+                nc,
+                x_grouped[g][:].rearrange("p (c i) t -> p c t i", i=4),
+                picked[g][:].rearrange("p t (c i) -> p c t i", i=4),
+                CUT_X,
+            )
+
+        def quantise_tokens(g):
+            nc.vector.quantize_mx(
+                out=x_codes[g][:].bitcast(FP8X4),
+                scales=x_scales[g][:],
+                in_=x_grouped[g][:].rearrange("p c t -> p (c t)"),
+            )
+
+        for g in range(PASSES):
+            picked.append(held.tile([P, PACK, SLOTS], F32, name="picked%d" % g))
+            x_grouped.append(held.tile([P, SLOTS, PACK], BF16, name="x_grouped%d" % g, align_bytes=64))
+            x_codes.append(held.tile([P, SLOTS], U32, name="x_codes%d" % g, align_bytes=64))
+            x_scales.append(held.tile([P, SLOTS], U8, name="x_scales%d" % g, align_bytes=64))
+
+        for t in range(PACK):
+            gather_plane(0, t)
+        interleave_tokens(0)
+        gather_plane(1, 0)
+        quantise_tokens(0)
+        for t in range(1, PACK):
+            gather_plane(1, t)
+        interleave_tokens(1)
+
+        units = []
+        for pair in range(PAIRS):
+            for e in (2 * pair, 2 * pair + 1):
+                for kind in ("w1", "w3"):
+                    for g in range(PASSES):
+                        units.append((kind, e, g))
+            if pair == 0:
+                units.append(("gate", pair, 0))
+            units.append(("w2", 2 * pair, 0))
+            units.append(("w2", 2 * pair + 1, 0))
+            if pair == 1:
+                units.append(("gate", pair, 0))
+
+        gate_view = gate.rearrange("(b p) s -> p b s", p=P)
+        gate_sb = {}
+        w_codes = {}
+        w_scales = {}
+        grouped_of = {}
+        h_codes = {}
+        h_scales = {}
+        gelu_of = {}
+        hidden_of = {}
+        acc_of = {}
+        y_of = {}
+        sources = {"w1": w1, "w3": w3}
+        after_copy = {0: [lambda: quantise_tokens(1)]}
+        after_quant = {}
+
+        def at(table, step, action):
+            table.setdefault(step, []).append(action)
+
+        def load_and_interleave(unit):
+            kind, e, g = unit
+            if kind == "gate":
+                gate_sb[e] = held.tile([P, N_BLOCKS, PAIR], F32, name="gate_sb%d" % e)
+                nc.sync.dma_start(gate_sb[e][:], gate_view[:, :, e * PAIR:(e + 1) * PAIR])
+            elif kind == "w2":
+                raw = ring.tile([P, PACK, N], F32, name="raw2", tag="raw")
+                nc.sync.dma_start(raw[:], w2[e].rearrange("(p j) n -> p j n", j=PACK))
+                grouped = stage.tile([P, N * PACK], BF16, name="grouped2", tag="grouped", align_bytes=64)
+                shared_copy(
+                    nc,
+                    grouped[:].rearrange("p (n i j) -> p n j i", i=4, j=PACK),
+                    raw[:].rearrange("p j (n i) -> p n j i", i=4),
+                    CUT_W2[e],
+                )
+                grouped_of[unit] = grouped
+            else:
+                raw = ring.tile([P, PACK, H], F32, name="raw", tag="raw")
+                rows = sources[kind][e, g * K_PASS:(g + 1) * K_PASS, :]
+                nc.sync.dma_start(raw[:], rows.rearrange("(p j) c -> p j c", j=PACK))
+                grouped = stage.tile([P, H * PACK], BF16, name="grouped", tag="grouped", align_bytes=64)
+                dst = grouped[:].rearrange("p (t m j) -> p m j t", t=4, j=PACK)
+                src = raw[:].rearrange("p j (m t) -> p m j t", t=4)
+                if unit == LAST_UNIT:
+                    for t0 in (0, 2):
+                        shared_copy(nc, dst[:, :, :, t0:t0 + 2], src[:, :, :, t0:t0 + 2], CUT_W_LAST)
+                else:
+                    shared_copy(nc, dst, src, CUT_W[e])
+                grouped_of[unit] = grouped
+
+        def first_layer(kind, e):
+            acc = psum.tile([P, 4, C], F32, name="acc_" + kind, tag="acc_" + kind)
+            for t in range(4):
+                for g in range(PASSES):
+                    cols = slice(t * P, (t + 1) * P)
+                    slots = slice(e * C, (e + 1) * C)
+                    nc.tensor.matmul_mx(
+                        out=acc[:, t, :],
+                        lhsT=w_codes[(kind, e, g)][:, cols].bitcast(FP8X4),
+                        lhsT_scale=w_scales[(kind, e, g)][:, cols],
+                        rhs=x_codes[g][:, slots].bitcast(FP8X4),
+                        rhs_scale=x_scales[g][:, slots],
+                        start=(g == 0),
+                        stop=(g == PASSES - 1),
+                    )
+            acc_of[(kind, e)] = acc
+
+        def gelu_step(e):
+            gelu = work.tile([P, 4, C], F32, name="gelu")
+            nc.scalar.activation(out=gelu[:], in_=acc_of[("w1", e)][:], func=GELU)
+            gelu_of[e] = gelu
+
+        def product_step(e):
+            hidden = work.tile([P, C, 4], BF16, name="hidden", align_bytes=64)
+            nc.vector.tensor_tensor(
+                out=hidden[:],
+                in0=gelu_of[e][:].rearrange("p t c -> p c t"),
+                in1=acc_of[("w3", e)][:].rearrange("p t c -> p c t"),
+                op=MULT,
+            )
+            hidden_of[e] = hidden
+
+        def quantise_hidden(e, step):
+            codes = held.tile([P, C], U32, name="h_codes%d" % e, align_bytes=64)
+            scales = held.tile([P, C], U8, name="h_scales%d" % e, align_bytes=64)
+            nc.vector.quantize_mx(
+                out=codes[:].bitcast(FP8X4),
+                scales=scales[:],
+                in_=hidden_of[e][:].rearrange("p c t -> p (c t)"),
+            )
+            h_codes[e] = codes
+            h_scales[e] = scales
+            second_layer(e, step)
+
+        def weigh(e, nb):
+            pair = e // 2
+            if e % 2 == 0:
+                y_of[(pair, nb)] = held.tile([P, PAIR], F32, name="y_sb%d_%d" % (pair, nb))
+            half = slice((e % 2) * C, (e % 2 + 1) * C)
+            nc.vector.tensor_tensor(
+                out=y_of[(pair, nb)][:, half],
+                in0=acc_of[("y", e, nb)][:],
+                in1=gate_sb[pair][:, nb, half],
+                op=MULT,
+            )
+
+        def scatter(pair, nb):
+            nc.vector.tensor_copy(
+                windows[nb][:].indirect(offsets[:, pair * (PAIR // 16):(pair + 1) * (PAIR // 16)]),
+                y_of[(pair, nb)][:],
+            )
+            if pair == PAIRS - 1:
+                nc.sync.dma_start(out[nb * P:(nb + 1) * P, :], windows[nb][:])
+
+        def second_layer(e, step):
+            if e not in h_codes or ("w2", e, 0) not in w_codes:
+                return
+            for nb in range(N_BLOCKS):
+                cols = slice(nb * P, (nb + 1) * P)
+                acc = psum.tile([P, C], F32, name="acc_y", tag="acc_y", bufs=4)
+                acc_of[("y", e, nb)] = acc
+                nc.tensor.matmul_mx(
+                    out=acc[:],
+                    lhsT=w_codes[("w2", e, 0)][:, cols].bitcast(FP8X4),
+                    lhsT_scale=w_scales[("w2", e, 0)][:, cols],
+                    rhs=h_codes[e][:].bitcast(FP8X4),
+                    rhs_scale=h_scales[e][:],
+                    start=True,
+                    stop=True,
+                )
+            gate_step = units.index(("gate", e // 2, 0))
+            for nb in range(N_BLOCKS):
+                when = max(step + SCATTER_STEPS[nb], gate_step)
+                at(after_quant, when, lambda nb=nb: weigh(e, nb))
+                if e % 2 == 1:
+                    at(after_quant, when, lambda nb=nb: scatter(e // 2, nb))
+
+        def quantise(unit, step):
+            kind, e, g = unit
+            if kind == "gate":
+                return
+            width = N if kind == "w2" else H
+            codes = held.tile([P, width], U32, name="c_%s_%d_%d" % unit, align_bytes=64)
+            scales = held.tile([P, width], U8, name="s_%s_%d_%d" % unit, align_bytes=64)
+            pieces = 2 if unit == LAST_UNIT else 1
+            for piece in range(pieces):
+                cols = slice(piece * width // pieces, (piece + 1) * width // pieces)
+                wide = slice(piece * width * PACK // pieces, (piece + 1) * width * PACK // pieces)
+                nc.vector.quantize_mx(
+                    out=codes[:, cols].bitcast(FP8X4), scales=scales[:, cols], in_=grouped_of[unit][:, wide]
+                )
+            w_codes[unit] = codes
+            w_scales[unit] = scales
+            if kind == "w1" and g == PASSES - 1:
+                first_layer(kind, e)
+                at(after_copy, step + 1, lambda: gelu_step(e))
+            if kind == "w3" and g == PASSES - 1:
+                first_layer(kind, e)
+                at(after_quant, step + 1, lambda: product_step(e))
+                at(after_quant, step + 2, lambda: quantise_hidden(e, step + 2))
+            if kind == "w2":
+                second_layer(e, step)
+
+        direct_from = len(units) - DIRECT_UNITS
+        for step in range(len(units) + 8):
+            if step < len(units):
+                load_and_interleave(units[step])
+            for action in after_copy.get(step, []):
+                action()
+            if 1 <= step <= direct_from:
+                quantise(units[step - 1], step)
+            if direct_from <= step < len(units):
+                quantise(units[step], step)
+            for action in after_quant.get(step, []):
+                action()

@@ -24,7 +24,7 @@ PAIRS = E // 2
 N_BLOCKS = N // P
 
 RING = 12
-CUT_W = (60, 60, 60, 60)
+CUT_W = (60, 60, 16, 44)
 CUT_W_LAST = 84
 CUT_X = 78
 CUT_W2 = (24, 24, 0, 0)

@@ -27,7 +27,7 @@ RING = 12
 CUT_W = (60, 60, 16, 44)
 CUT_W_LAST = 84
 CUT_X = 78
-CUT_W2 = (24, 24, 0, 0)
+CUT_W2 = (24, 24, 0, 32)
 SCATTER_STEPS = (1, 2)
 LAST_UNIT = ("w3", E - 1, PASSES - 1)
 DIRECT_UNITS = 5

@@ -122,6 +122,7 @@ def tile_routed_moe_kernel(tc, xT, w1, w3, w2, gate, offs, out):
         w_codes = {}
         w_scales = {}
         grouped_of = {}
+        raw_of = {}
         h_codes = {}
         h_scales = {}
         gelu_of = {}
@@ -155,6 +156,7 @@ def tile_routed_moe_kernel(tc, xT, w1, w3, w2, gate, offs, out):
                 raw = ring.tile([P, PACK, H], F32, name="raw", tag="raw")
                 rows = sources[kind][e, g * K_PASS:(g + 1) * K_PASS, :]
                 nc.sync.dma_start(raw[:], rows.rearrange("(p j) c -> p j c", j=PACK))
+                raw_of[unit] = raw
                 grouped = stage.tile([P, H * PACK], BF16, name="grouped", tag="grouped", align_bytes=64)
                 dst = grouped[:].rearrange("p (t m j) -> p m j t", t=4, j=PACK)
                 src = raw[:].rearrange("p j (m t) -> p m j t", t=4)
@@ -183,15 +185,15 @@ def tile_routed_moe_kernel(tc, xT, w1, w3, w2, gate, offs, out):
             acc_of[(kind, e)] = acc
 
         def gelu_step(e):
-            gelu = work.tile([P, 4, C], F32, name="gelu")
-            nc.scalar.activation(out=gelu[:], in_=acc_of[("w1", e)][:], func=GELU)
+            gelu = raw_of[("w3", e, PASSES - 1)][:, 0, :].rearrange("p (t c) -> p t c", t=4)
+            nc.scalar.activation(out=gelu, in_=acc_of[("w1", e)][:], func=GELU)
             gelu_of[e] = gelu
 
         def product_step(e):
             hidden = work.tile([P, C, 4], BF16, name="hidden", align_bytes=64)
             nc.vector.tensor_tensor(
                 out=hidden[:],
-                in0=gelu_of[e][:].rearrange("p t c -> p c t"),
+                in0=gelu_of[e].rearrange("p t c -> p c t"),
                 in1=acc_of[("w3", e)][:].rearrange("p t c -> p c t"),
                 op=MULT,
             )

@@ -23,7 +23,8 @@ PAIR = 2 * C
 PAIRS = E // 2
 N_BLOCKS = N // P
 
-RING = 12
+RING = 7
+MERGED_EXPERTS = 2
 CUT_W = (60, 60, 16, 44)
 CUT_W_LAST = 84
 CUT_X = 78
@@ -63,16 +64,17 @@ def tile_routed_moe_kernel(tc, xT, w1, w3, w2, gate, offs, out):
             nc.vector.memset(window[:], 0.0)
             windows.append(window)
 
-        x_planes = xT.rearrange("(g p t) n -> g t p n", p=P, t=PACK)
+        x_rows = xT.rearrange("(g p t) n -> g p t n", p=P, t=PACK)
         x_codes = []
         x_scales = []
         x_grouped = []
         picked = []
 
-        def gather_plane(g, t):
-            plane = ring.tile([P, T], F32, name="plane", tag="raw")
-            nc.sync.dma_start(plane[:], x_planes[g, t])
-            nc.vector.tensor_copy(picked[g][:, t, :], plane[:].indirect(offsets[:]))
+        def gather_planes(g, t0):
+            planes = ring.tile([P, 2, T], F32, name="planes", tag="raw")
+            nc.sync.dma_start(planes[:], x_rows[g, :, t0:t0 + 2, :])
+            for t in (t0, t0 + 1):
+                nc.vector.tensor_copy(picked[g][:, t, :], planes[:, t - t0, :].indirect(offsets[:]))
 
         def interleave_tokens(g):
             shared_copy(
@@ -95,13 +97,12 @@ def tile_routed_moe_kernel(tc, xT, w1, w3, w2, gate, offs, out):
             x_codes.append(held.tile([P, SLOTS], U32, name="x_codes%d" % g, align_bytes=64))
             x_scales.append(held.tile([P, SLOTS], U8, name="x_scales%d" % g, align_bytes=64))
 
-        for t in range(PACK):
-            gather_plane(0, t)
+        gather_planes(0, 0)
+        gather_planes(0, 2)
         interleave_tokens(0)
-        gather_plane(1, 0)
+        gather_planes(1, 0)
         quantise_tokens(0)
-        for t in range(1, PACK):
-            gather_plane(1, t)
+        gather_planes(1, 2)
         interleave_tokens(1)
 
         units = []
@@ -130,6 +131,7 @@ def tile_routed_moe_kernel(tc, xT, w1, w3, w2, gate, offs, out):
         acc_of = {}
         y_of = {}
         sources = {"w1": w1, "w3": w3}
+        merged_raw = {}
         after_copy = {0: [lambda: quantise_tokens(1)]}
         after_quant = {}
 
@@ -142,24 +144,40 @@ def tile_routed_moe_kernel(tc, xT, w1, w3, w2, gate, offs, out):
                 gate_sb[e] = held.tile([P, N_BLOCKS, PAIR], F32, name="gate_sb%d" % e)
                 nc.sync.dma_start(gate_sb[e][:], gate_view[:, :, e * PAIR:(e + 1) * PAIR])
             elif kind == "w2":
-                raw = ring.tile([P, PACK, N], F32, name="raw2", tag="raw")
-                nc.sync.dma_start(raw[:], w2[e].rearrange("(p j) n -> p j n", j=PACK))
+                if e < MERGED_EXPERTS:
+                    if e % 2 == 0:
+                        both = ring.tile([P, 2, PACK, N], F32, name="raw2_both", tag="raw")
+                        nc.sync.dma_start(both[:], w2[e:e + 2].rearrange("e (p j) n -> p e j n", j=PACK))
+                        merged_raw[kind] = both
+                    raw = merged_raw[kind][:, e % 2]
+                else:
+                    single = ring.tile([P, PACK, N], F32, name="raw2", tag="raw")
+                    nc.sync.dma_start(single[:], w2[e].rearrange("(p j) n -> p j n", j=PACK))
+                    raw = single[:]
                 grouped = stage.tile([P, N * PACK], BF16, name="grouped2", tag="grouped", align_bytes=64)
                 shared_copy(
                     nc,
                     grouped[:].rearrange("p (n i j) -> p n j i", i=4, j=PACK),
-                    raw[:].rearrange("p j (n i) -> p n j i", i=4),
+                    raw.rearrange("p j (n i) -> p n j i", i=4),
                     CUT_W2[e],
                 )
                 grouped_of[unit] = grouped
             else:
-                raw = ring.tile([P, PACK, H], F32, name="raw", tag="raw")
-                rows = sources[kind][e, g * K_PASS:(g + 1) * K_PASS, :]
-                nc.sync.dma_start(raw[:], rows.rearrange("(p j) c -> p j c", j=PACK))
-                raw_of[unit] = raw
+                if e < MERGED_EXPERTS:
+                    if g == 0:
+                        both = ring.tile([P, PASSES, PACK, H], F32, name="raw_both", tag="raw")
+                        nc.sync.dma_start(both[:], sources[kind][e].rearrange("(g p j) c -> p g j c", p=P, j=PACK))
+                        merged_raw[kind] = both
+                    raw = merged_raw[kind][:, g]
+                else:
+                    single = ring.tile([P, PACK, H], F32, name="raw", tag="raw")
+                    rows = sources[kind][e, g * K_PASS:(g + 1) * K_PASS, :]
+                    nc.sync.dma_start(single[:], rows.rearrange("(p j) c -> p j c", j=PACK))
+                    raw = single[:]
                 grouped = stage.tile([P, H * PACK], BF16, name="grouped", tag="grouped", align_bytes=64)
                 dst = grouped[:].rearrange("p (t m j) -> p m j t", t=4, j=PACK)
-                src = raw[:].rearrange("p j (m t) -> p m j t", t=4)
+                src = raw.rearrange("p j (m t) -> p m j t", t=4)
+                raw_of[unit] = raw
                 if unit == LAST_UNIT:
                     for t0 in (0, 2):
                         shared_copy(nc, dst[:, :, :, t0:t0 + 2], src[:, :, :, t0:t0 + 2], CUT_W_LAST)

@@ -23,7 +23,6 @@ PAIR = 2 * C
 PAIRS = E // 2
 N_BLOCKS = N // P
 
-RING = 7
 MERGED_EXPERTS = 2
 CUT_W = (60, 60, 16, 44)
 CUT_W_LAST = 84
@@ -46,13 +45,13 @@ def tile_routed_moe_kernel(tc, xT, w1, w3, w2, gate, offs, out):
     nc = tc.nc
     with ExitStack() as ctx:
         held = ctx.enter_context(tc.tile_pool(name="held", bufs=1))
-        ring = ctx.enter_context(tc.tile_pool(name="ring", bufs=RING))
+        big = ctx.enter_context(tc.tile_pool(name="big", bufs=3))
+        small = ctx.enter_context(tc.tile_pool(name="small", bufs=2))
         stage = ctx.enter_context(tc.tile_pool(name="stage", bufs=4))
         work = ctx.enter_context(tc.tile_pool(name="work", bufs=2))
         psum = ctx.enter_context(tc.psum_pool(name="psum", bufs=2))
 
         offsets = held.tile([P, SLOTS // 16], U16, name="offsets")
-        nc.sync.dma_start(offsets[:], offs)
 
         warm = held.tile([P, 2], F32, name="warm")
         nc.vector.memset(warm[:], 0.0)
@@ -70,11 +69,13 @@ def tile_routed_moe_kernel(tc, xT, w1, w3, w2, gate, offs, out):
         x_grouped = []
         picked = []
 
-        def gather_planes(g, t0):
-            planes = ring.tile([P, 2, T], F32, name="planes", tag="raw")
-            nc.sync.dma_start(planes[:], x_rows[g, :, t0:t0 + 2, :])
-            for t in (t0, t0 + 1):
-                nc.vector.tensor_copy(picked[g][:, t, :], planes[:, t - t0, :].indirect(offsets[:]))
+        def gather_planes(g):
+            planes = big.tile([P, PACK, T], F32, name="planes", tag="big")
+            nc.sync.dma_start(planes[:], x_rows[g])
+            if g == 0:
+                nc.sync.dma_start(offsets[:], offs)
+            for t in range(PACK):
+                nc.vector.tensor_copy(picked[g][:, t, :], planes[:, t, :].indirect(offsets[:]))
 
         def interleave_tokens(g):
             shared_copy(
@@ -97,12 +98,10 @@ def tile_routed_moe_kernel(tc, xT, w1, w3, w2, gate, offs, out):
             x_codes.append(held.tile([P, SLOTS], U32, name="x_codes%d" % g, align_bytes=64))
             x_scales.append(held.tile([P, SLOTS], U8, name="x_scales%d" % g, align_bytes=64))
 
-        gather_planes(0, 0)
-        gather_planes(0, 2)
+        gather_planes(0)
         interleave_tokens(0)
-        gather_planes(1, 0)
         quantise_tokens(0)
-        gather_planes(1, 2)
+        gather_planes(1)
         interleave_tokens(1)
 
         units = []
@@ -146,12 +145,12 @@ def tile_routed_moe_kernel(tc, xT, w1, w3, w2, gate, offs, out):
             elif kind == "w2":
                 if e < MERGED_EXPERTS:
                     if e % 2 == 0:
-                        both = ring.tile([P, 2, PACK, N], F32, name="raw2_both", tag="raw")
+                        both = small.tile([P, 2, PACK, N], F32, name="raw2_both", tag="small")
                         nc.sync.dma_start(both[:], w2[e:e + 2].rearrange("e (p j) n -> p e j n", j=PACK))
                         merged_raw[kind] = both
                     raw = merged_raw[kind][:, e % 2]
                 else:
-                    single = ring.tile([P, PACK, N], F32, name="raw2", tag="raw")
+                    single = small.tile([P, PACK, N], F32, name="raw2", tag="small")
                     nc.sync.dma_start(single[:], w2[e].rearrange("(p j) n -> p j n", j=PACK))
                     raw = single[:]
                 grouped = stage.tile([P, N * PACK], BF16, name="grouped2", tag="grouped", align_bytes=64)
@@ -163,17 +162,16 @@ def tile_routed_moe_kernel(tc, xT, w1, w3, w2, gate, offs, out):
                 )
                 grouped_of[unit] = grouped
             else:
+                if kind == "w1" and g == 0:
+                    merged_raw["w"] = big.tile([P, 2, PASSES, PACK, H], F32, name="raw", tag="big")
+                matrix = merged_raw["w"][:, ("w1", "w3").index(kind)]
+                rows = sources[kind][e].rearrange("(g p j) c -> p g j c", p=P, j=PACK)
                 if e < MERGED_EXPERTS:
                     if g == 0:
-                        both = ring.tile([P, PASSES, PACK, H], F32, name="raw_both", tag="raw")
-                        nc.sync.dma_start(both[:], sources[kind][e].rearrange("(g p j) c -> p g j c", p=P, j=PACK))
-                        merged_raw[kind] = both
-                    raw = merged_raw[kind][:, g]
+                        nc.sync.dma_start(matrix, rows)
                 else:
-                    single = ring.tile([P, PACK, H], F32, name="raw", tag="raw")
-                    rows = sources[kind][e, g * K_PASS:(g + 1) * K_PASS, :]
-                    nc.sync.dma_start(single[:], rows.rearrange("(p j) c -> p j c", j=PACK))
-                    raw = single[:]
+                    nc.sync.dma_start(matrix[:, g], rows[:, g])
+                raw = matrix[:, g]
                 grouped = stage.tile([P, H * PACK], BF16, name="grouped", tag="grouped", align_bytes=64)
                 dst = grouped[:].rearrange("p (t m j) -> p m j t", t=4, j=PACK)
                 src = raw.rearrange("p j (m t) -> p m j t", t=4)

@@ -29,6 +29,7 @@ CUT_W_LAST = 84
 CUT_X = 78
 CUT_W2 = (24, 24, 0, 32)
 SCATTER_STEPS = (1, 2)
+LAST_W2 = ("w2", E - 1, 0)
 LAST_UNIT = ("w3", E - 1, PASSES - 1)
 DIRECT_UNITS = 5
 
@@ -277,7 +278,7 @@ def tile_routed_moe_kernel(tc, xT, w1, w3, w2, gate, offs, out):
             width = N if kind == "w2" else H
             codes = held.tile([P, width], U32, name="c_%s_%d_%d" % unit, align_bytes=64)
             scales = held.tile([P, width], U8, name="s_%s_%d_%d" % unit, align_bytes=64)
-            pieces = 2 if unit == LAST_UNIT else 1
+            pieces = 2 if unit in (LAST_UNIT, LAST_W2) else 1
             for piece in range(pieces):
                 cols = slice(piece * width // pieces, (piece + 1) * width // pieces)
                 wide = slice(piece * width * PACK // pieces, (piece + 1) * width * PACK // pieces)

@@ -185,13 +185,16 @@ def tile_routed_moe_kernel(tc, xT, w1, w3, w2, gate, offs, out):
                 grouped_of[unit] = grouped
 
         def first_layer(kind, e):
-            acc = psum.tile([P, 4, C], F32, name="acc_" + kind, tag="acc_" + kind)
+            parts = 2 if (kind, e) == LAST_UNIT[:2] else 1
+            accs = []
+            for part in range(parts):
+                accs.append(psum.tile([P, 4 // parts, C], F32, name="acc_" + kind, tag="acc_" + kind))
             for t in range(4):
                 for g in range(PASSES):
                     cols = slice(t * P, (t + 1) * P)
                     slots = slice(e * C, (e + 1) * C)
                     nc.tensor.matmul_mx(
-                        out=acc[:, t, :],
+                        out=accs[t * parts // 4][:, t % (4 // parts), :],
                         lhsT=w_codes[(kind, e, g)][:, cols].bitcast(FP8X4),
                         lhsT_scale=w_scales[(kind, e, g)][:, cols],
                         rhs=x_codes[g][:, slots].bitcast(FP8X4),
@@ -199,21 +202,24 @@ def tile_routed_moe_kernel(tc, xT, w1, w3, w2, gate, offs, out):
                         start=(g == 0),
                         stop=(g == PASSES - 1),
                     )
-            acc_of[(kind, e)] = acc
+            acc_of[(kind, e)] = accs
 
         def gelu_step(e):
             gelu = raw_of[("w3", e, PASSES - 1)][:, 0, :].rearrange("p (t c) -> p t c", t=4)
-            nc.scalar.activation(out=gelu, in_=acc_of[("w1", e)][:], func=GELU)
+            nc.scalar.activation(out=gelu, in_=acc_of[("w1", e)][0][:], func=GELU)
             gelu_of[e] = gelu
 
         def product_step(e):
             hidden = work.tile([P, C, 4], BF16, name="hidden", align_bytes=64)
-            nc.vector.tensor_tensor(
-                out=hidden[:],
-                in0=gelu_of[e].rearrange("p t c -> p c t"),
-                in1=acc_of[("w3", e)][:].rearrange("p t c -> p c t"),
-                op=MULT,
-            )
+            accs = acc_of[("w3", e)]
+            for part in range(len(accs)):
+                ts = slice(part * 4 // len(accs), (part + 1) * 4 // len(accs))
+                nc.vector.tensor_tensor(
+                    out=hidden[:, :, ts],
+                    in0=gelu_of[e][:, ts, :].rearrange("p t c -> p c t"),
+                    in1=accs[part][:].rearrange("p t c -> p c t"),
+                    op=MULT,
+                )
             hidden_of[e] = hidden
 
         def quantise_hidden(e, step):

@@ -155,12 +155,14 @@ def tile_routed_moe_kernel(tc, xT, w1, w3, w2, gate, offs, out):
                     nc.sync.dma_start(single[:], w2[e].rearrange("(p j) n -> p j n", j=PACK))
                     raw = single[:]
                 grouped = stage.tile([P, N * PACK], BF16, name="grouped2", tag="grouped", align_bytes=64)
-                shared_copy(
-                    nc,
-                    grouped[:].rearrange("p (n i j) -> p n j i", i=4, j=PACK),
-                    raw.rearrange("p j (n i) -> p n j i", i=4),
-                    CUT_W2[e],
-                )
+                dst = grouped[:].rearrange("p (n i j) -> p n j i", i=4, j=PACK)
+                src = raw.rearrange("p j (n i) -> p n j i", i=4)
+                if unit == LAST_W2:
+                    for nb in range(N_BLOCKS):
+                        rows = slice(nb * P // 4, (nb + 1) * P // 4)
+                        shared_copy(nc, dst[:, rows], src[:, rows], 0)
+                else:
+                    shared_copy(nc, dst, src, CUT_W2[e])
                 grouped_of[unit] = grouped
             else:
                 if kind == "w1" and g == 0:

from contextlib import ExitStack

import concourse.mybir as mybir

K, T, E, C, H, N = 1024, 2048, 4, 128, 512, 256
FLOPS = 2 * E * C * (2 * K * H + H * N)

F32 = mybir.dt.float32
BF16 = mybir.dt.bfloat16
U32 = mybir.dt.uint32
U16 = mybir.dt.uint16
U8 = mybir.dt.uint8
FP8X4 = mybir.dt.float8_e4m3fn_x4
GELU = mybir.ActivationFunctionType.Gelu_apprx_tanh
MULT = mybir.AluOpType.mult

P = 128
PACK = 4
K_PASS = P * PACK
PASSES = K // K_PASS
SLOTS = E * C
PAIR = 2 * C
PAIRS = E // 2
N_BLOCKS = N // P

MERGED_EXPERTS = 2
CUT_W = (60, 60, 16, 44)
CUT_W_LAST = 84
CUT_X = 78
CUT_W2 = (24, 24, 0, 32)
SCATTER_STEPS = (1, 2)
LAST_W2 = ("w2", E - 1, 0)
LAST_UNIT = ("w3", E - 1, PASSES - 1)
DIRECT_UNITS = 5


def shared_copy(nc, dst, src, cut):
    rows = dst.shape[1]
    if cut > 0:
        nc.vector.tensor_copy(out=dst[:, :cut], in_=src[:, :cut])
    if cut < rows:
        nc.scalar.copy(out=dst[:, cut:], in_=src[:, cut:])


def tile_routed_moe_kernel(tc, xT, w1, w3, w2, gate, offs, out):
    nc = tc.nc
    with ExitStack() as ctx:
        held = ctx.enter_context(tc.tile_pool(name="held", bufs=1))
        big = ctx.enter_context(tc.tile_pool(name="big", bufs=3))
        small = ctx.enter_context(tc.tile_pool(name="small", bufs=2))
        stage = ctx.enter_context(tc.tile_pool(name="stage", bufs=4))
        work = ctx.enter_context(tc.tile_pool(name="work", bufs=2))
        psum = ctx.enter_context(tc.psum_pool(name="psum", bufs=2))

        offsets = held.tile([P, SLOTS // 16], U16, name="offsets")

        warm = held.tile([P, 2], F32, name="warm")
        nc.vector.memset(warm[:], 0.0)
        nc.scalar.activation(out=warm[:, 1:2], in_=warm[:, 0:1], func=GELU)

        windows = []
        for nb in range(N_BLOCKS):
            window = held.tile([P, T], F32, name="window%d" % nb)
            nc.vector.memset(window[:], 0.0)
            windows.append(window)

        x_rows = xT.rearrange("(g p t) n -> g p t n", p=P, t=PACK)
        x_codes = []
        x_scales = []
        x_grouped = []
        picked = []

        def gather_planes(g):
            planes = big.tile([P, PACK, T], F32, name="planes", tag="big")
            nc.sync.dma_start(planes[:], x_rows[g])
            if g == 0:
                nc.sync.dma_start(offsets[:], offs)
            for t in range(PACK):
                nc.vector.tensor_copy(picked[g][:, t, :], planes[:, t, :].indirect(offsets[:]))

        def interleave_tokens(g):
            shared_copy(
                nc,
                x_grouped[g][:].rearrange("p (c i) t -> p c t i", i=4),
                picked[g][:].rearrange("p t (c i) -> p c t i", i=4),
                CUT_X,
            )

        def quantise_tokens(g):
            nc.vector.quantize_mx(
                out=x_codes[g][:].bitcast(FP8X4),
                scales=x_scales[g][:],
                in_=x_grouped[g][:].rearrange("p c t -> p (c t)"),
            )

        for g in range(PASSES):
            picked.append(held.tile([P, PACK, SLOTS], F32, name="picked%d" % g))
            x_grouped.append(held.tile([P, SLOTS, PACK], BF16, name="x_grouped%d" % g, align_bytes=64))
            x_codes.append(held.tile([P, SLOTS], U32, name="x_codes%d" % g, align_bytes=64))
            x_scales.append(held.tile([P, SLOTS], U8, name="x_scales%d" % g, align_bytes=64))

        gather_planes(0)
        interleave_tokens(0)
        quantise_tokens(0)
        gather_planes(1)
        interleave_tokens(1)

        units = []
        for pair in range(PAIRS):
            for e in (2 * pair, 2 * pair + 1):
                for kind in ("w1", "w3"):
                    for g in range(PASSES):
                        units.append((kind, e, g))
            if pair == 0:
                units.append(("gate", pair, 0))
            units.append(("w2", 2 * pair, 0))
            units.append(("w2", 2 * pair + 1, 0))
            if pair == 1:
                units.append(("gate", pair, 0))

        gate_view = gate.rearrange("(b p) s -> p b s", p=P)
        gate_sb = {}
        w_codes = {}
        w_scales = {}
        grouped_of = {}
        raw_of = {}
        h_codes = {}
        h_scales = {}
        gelu_of = {}
        hidden_of = {}
        acc_of = {}
        y_of = {}
        sources = {"w1": w1, "w3": w3}
        merged_raw = {}
        after_copy = {0: [lambda: quantise_tokens(1)]}
        after_quant = {}

        def at(table, step, action):
            table.setdefault(step, []).append(action)

        def load_and_interleave(unit):
            kind, e, g = unit
            if kind == "gate":
                gate_sb[e] = held.tile([P, N_BLOCKS, PAIR], F32, name="gate_sb%d" % e)
                nc.sync.dma_start(gate_sb[e][:], gate_view[:, :, e * PAIR:(e + 1) * PAIR])
            elif kind == "w2":
                if e < MERGED_EXPERTS:
                    if e % 2 == 0:
                        both = small.tile([P, 2, PACK, N], F32, name="raw2_both", tag="small")
                        nc.sync.dma_start(both[:], w2[e:e + 2].rearrange("e (p j) n -> p e j n", j=PACK))
                        merged_raw[kind] = both
                    raw = merged_raw[kind][:, e % 2]
                else:
                    single = small.tile([P, PACK, N], F32, name="raw2", tag="small")
                    nc.sync.dma_start(single[:], w2[e].rearrange("(p j) n -> p j n", j=PACK))
                    raw = single[:]
                grouped = stage.tile([P, N * PACK], BF16, name="grouped2", tag="grouped", align_bytes=64)
                dst = grouped[:].rearrange("p (n i j) -> p n j i", i=4, j=PACK)
                src = raw.rearrange("p j (n i) -> p n j i", i=4)
                if unit == LAST_W2:
                    for nb in range(N_BLOCKS):
                        rows = slice(nb * P // 4, (nb + 1) * P // 4)
                        shared_copy(nc, dst[:, rows], src[:, rows], 0)
                else:
                    shared_copy(nc, dst, src, CUT_W2[e])
                grouped_of[unit] = grouped
            else:
                if kind == "w1" and g == 0:
                    merged_raw["w"] = big.tile([P, 2, PASSES, PACK, H], F32, name="raw", tag="big")
                matrix = merged_raw["w"][:, ("w1", "w3").index(kind)]
                rows = sources[kind][e].rearrange("(g p j) c -> p g j c", p=P, j=PACK)
                if e < MERGED_EXPERTS:
                    if g == 0:
                        nc.sync.dma_start(matrix, rows)
                else:
                    nc.sync.dma_start(matrix[:, g], rows[:, g])
                raw = matrix[:, g]
                grouped = stage.tile([P, H * PACK], BF16, name="grouped", tag="grouped", align_bytes=64)
                dst = grouped[:].rearrange("p (t m j) -> p m j t", t=4, j=PACK)
                src = raw.rearrange("p j (m t) -> p m j t", t=4)
                raw_of[unit] = raw
                if unit == LAST_UNIT:
                    for t0 in (0, 2):
                        shared_copy(nc, dst[:, :, :, t0:t0 + 2], src[:, :, :, t0:t0 + 2], CUT_W_LAST)
                else:
                    shared_copy(nc, dst, src, CUT_W[e])
                grouped_of[unit] = grouped

        def first_layer(kind, e):
            parts = 2 if (kind, e) == LAST_UNIT[:2] else 1
            accs = []
            for part in range(parts):
                accs.append(psum.tile([P, 4 // parts, C], F32, name="acc_" + kind, tag="acc_" + kind))
            for t in range(4):
                for g in range(PASSES):
                    cols = slice(t * P, (t + 1) * P)
                    slots = slice(e * C, (e + 1) * C)
                    nc.tensor.matmul_mx(
                        out=accs[t * parts // 4][:, t % (4 // parts), :],
                        lhsT=w_codes[(kind, e, g)][:, cols].bitcast(FP8X4),
                        lhsT_scale=w_scales[(kind, e, g)][:, cols],
                        rhs=x_codes[g][:, slots].bitcast(FP8X4),
                        rhs_scale=x_scales[g][:, slots],
                        start=(g == 0),
                        stop=(g == PASSES - 1),
                    )
            acc_of[(kind, e)] = accs

        def gelu_step(e):
            gelu = raw_of[("w3", e, PASSES - 1)][:, 0, :].rearrange("p (t c) -> p t c", t=4)
            nc.scalar.activation(out=gelu, in_=acc_of[("w1", e)][0][:], func=GELU)
            gelu_of[e] = gelu

        def product_step(e):
            hidden = work.tile([P, C, 4], BF16, name="hidden", align_bytes=64)
            accs = acc_of[("w3", e)]
            for part in range(len(accs)):
                ts = slice(part * 4 // len(accs), (part + 1) * 4 // len(accs))
                nc.vector.tensor_tensor(
                    out=hidden[:, :, ts],
                    in0=gelu_of[e][:, ts, :].rearrange("p t c -> p c t"),
                    in1=accs[part][:].rearrange("p t c -> p c t"),
                    op=MULT,
                )
            hidden_of[e] = hidden

        def quantise_hidden(e, step):
            codes = held.tile([P, C], U32, name="h_codes%d" % e, align_bytes=64)
            scales = held.tile([P, C], U8, name="h_scales%d" % e, align_bytes=64)
            nc.vector.quantize_mx(
                out=codes[:].bitcast(FP8X4),
                scales=scales[:],
                in_=hidden_of[e][:].rearrange("p c t -> p (c t)"),
            )
            h_codes[e] = codes
            h_scales[e] = scales
            second_layer(e, step)

        def weigh(e, nb):
            pair = e // 2
            if e % 2 == 0:
                y_of[(pair, nb)] = held.tile([P, PAIR], F32, name="y_sb%d_%d" % (pair, nb))
            half = slice((e % 2) * C, (e % 2 + 1) * C)
            nc.vector.tensor_tensor(
                out=y_of[(pair, nb)][:, half],
                in0=acc_of[("y", e, nb)][:],
                in1=gate_sb[pair][:, nb, half],
                op=MULT,
            )

        def scatter(pair, nb):
            nc.vector.tensor_copy(
                windows[nb][:].indirect(offsets[:, pair * (PAIR // 16):(pair + 1) * (PAIR // 16)]),
                y_of[(pair, nb)][:],
            )
            if pair == PAIRS - 1:
                nc.sync.dma_start(out[nb * P:(nb + 1) * P, :], windows[nb][:])

        def second_layer(e, step):
            if e not in h_codes or ("w2", e, 0) not in w_codes:
                return
            for nb in range(N_BLOCKS):
                cols = slice(nb * P, (nb + 1) * P)
                acc = psum.tile([P, C], F32, name="acc_y", tag="acc_y", bufs=4)
                acc_of[("y", e, nb)] = acc
                nc.tensor.matmul_mx(
                    out=acc[:],
                    lhsT=w_codes[("w2", e, 0)][:, cols].bitcast(FP8X4),
                    lhsT_scale=w_scales[("w2", e, 0)][:, cols],
                    rhs=h_codes[e][:].bitcast(FP8X4),
                    rhs_scale=h_scales[e][:],
                    start=True,
                    stop=True,
                )
            gate_step = units.index(("gate", e // 2, 0))
            for nb in range(N_BLOCKS):
                when = max(step + SCATTER_STEPS[nb], gate_step)
                at(after_quant, when, lambda nb=nb: weigh(e, nb))
                if e % 2 == 1:
                    at(after_quant, when, lambda nb=nb: scatter(e // 2, nb))

        def quantise(unit, step):
            kind, e, g = unit
            if kind == "gate":
                return
            width = N if kind == "w2" else H
            codes = held.tile([P, width], U32, name="c_%s_%d_%d" % unit, align_bytes=64)
            scales = held.tile([P, width], U8, name="s_%s_%d_%d" % unit, align_bytes=64)
            pieces = 2 if unit in (LAST_UNIT, LAST_W2) else 1
            for piece in range(pieces):
                cols = slice(piece * width // pieces, (piece + 1) * width // pieces)
                wide = slice(piece * width * PACK // pieces, (piece + 1) * width * PACK // pieces)
                nc.vector.quantize_mx(
                    out=codes[:, cols].bitcast(FP8X4), scales=scales[:, cols], in_=grouped_of[unit][:, wide]
                )
            w_codes[unit] = codes
            w_scales[unit] = scales
            if kind == "w1" and g == PASSES - 1:
                first_layer(kind, e)
                at(after_copy, step + 1, lambda: gelu_step(e))
            if kind == "w3" and g == PASSES - 1:
                first_layer(kind, e)
                at(after_quant, step + 1, lambda: product_step(e))
                at(after_quant, step + 2, lambda: quantise_hidden(e, step + 2))
            if kind == "w2":
                second_layer(e, step)

        direct_from = len(units) - DIRECT_UNITS
        for step in range(len(units) + 8):
            if step < len(units):
                load_and_interleave(units[step])
            for action in after_copy.get(step, []):
                action()
            if 1 <= step <= direct_from:
                quantise(units[step - 1], step)
            if direct_from <= step < len(units):
                quantise(units[step], step)
            for action in after_quant.get(step, []):
                action()
